import numpy as np
import ml_dtypes


def mxq(x, axis, fmt="e4m3"):
    dtype, down = {"e4m3": (ml_dtypes.float8_e4m3fn, 7), "e5m2": (ml_dtypes.float8_e5m2, 14)}[fmt]
    v = np.moveaxis(np.asarray(x, np.float32).astype(ml_dtypes.bfloat16).astype(np.float64), axis, -1)
    blocks = v.reshape(v.shape[:-1] + (-1, 32))
    amax = np.abs(blocks).max(-1, keepdims=True)
    byte = np.maximum(np.where(amax > 0, np.frexp(amax)[1] - 1 + 127, 0) - down, 1)
    scale = np.exp2(byte - 127.0)
    codes = (blocks / scale).astype(np.float32).astype(dtype).astype(np.float64)
    return np.moveaxis((codes * scale).reshape(v.shape), -1, axis)


WIDE = False


def mx_kscale(k):
    if not WIDE:
        return np.ones(k)
    levels = np.array([10, -10, 5, -5, 0])
    if k % 512:
        return np.exp2(np.random.permutation(np.resize(levels, k // 32))).repeat(32)
    a = np.empty((k // 512, 16))
    for p in range(k // 512):
        a[p, :8] = np.random.permutation(np.resize(levels, 8))
        for g in range(8):
            far = levels[np.abs(levels - a[p, g]) >= 10]
            a[p, g + 8] = far[np.random.randint(len(far))]
    return np.exp2(a.ravel()).repeat(32)


def f64(x):
    return np.asarray(x).astype(np.float64)


def striped(idx):
    return np.tile(idx.reshape(-1, 16).T, (8, 1)).astype(np.uint16)


def unstriped(offs):
    return offs[:16].T.reshape(-1).astype(np.int64)


def pack_weight(w):
    k, n = w.shape
    w = f64(np.asarray(w, np.float32).astype(ml_dtypes.bfloat16)).reshape(k // 32, 32, n)
    amax = np.abs(w).max(1)
    byte = np.clip(np.where(amax > 0, np.frexp(amax)[1] - 1 + 127 - 7, 1), 1, 254)
    scaled = (w * np.exp2(127.0 - byte)[:, None, :]).reshape(k, n).astype(np.float32)
    words = np.ascontiguousarray(scaled.reshape(k // 512, 128, 4, n).transpose(0, 1, 3, 2)).astype(ml_dtypes.float8_e4m3fn).view(np.uint8)
    return words, np.ascontiguousarray(byte.astype(np.uint8).reshape(k // 512, 16, n))


def unpack_weight(words, scales):
    g, p, n, _ = words.shape
    vals = np.ascontiguousarray(words).view(ml_dtypes.float8_e4m3fn).astype(np.float64) * np.repeat(np.exp2(scales.astype(np.float64) - 127.0), 8, axis=1)[..., None]
    return vals.transpose(0, 1, 3, 2).reshape(g * 512, n)


E2M1 = np.array([0.0, 0.5, 1.0, 1.5, 2.0, 3.0, 4.0, 6.0, -0.0, -0.5, -1.0, -1.5, -2.0, -3.0, -4.0, -6.0])


def pack_fp4(w):
    k, n = w.shape
    w = f64(np.asarray(w, np.float32).astype(ml_dtypes.bfloat16)).reshape(k // 32, 32, n)
    amax = np.abs(w).max(1)
    mant, ex = np.frexp(amax / 6.0)
    byte = np.clip(np.where(amax > 0, np.where(mant > 0.5, ex, ex - 1) + 127, 1), 1, 254)
    scaled = (w * np.exp2(127.0 - byte)[:, None, :]).reshape(k, n).astype(np.float32)
    c = np.ascontiguousarray(scaled.reshape(k // 512, 128, 4, n).transpose(0, 1, 3, 2)).astype(ml_dtypes.float4_e2m1fn).view(np.uint8) & 0xF
    words = (c[..., 0::2] | (c[..., 1::2] << 4)).reshape(k // 512, 128, 2 * n)
    return np.ascontiguousarray(words), np.ascontiguousarray(byte.astype(np.uint8).reshape(k // 512, 16, n))


def unpack_fp4(words, scales):
    g, _, n = scales.shape
    words = np.ascontiguousarray(words).reshape(g, 128, n, 2)
    nib = np.empty((g, 128, n, 4), np.uint8)
    nib[..., 0::2] = words & 0xF
    nib[..., 1::2] = words >> 4
    vals = E2M1[nib] * np.repeat(np.exp2(scales.astype(np.float64) - 127.0), 8, axis=1)[..., None]
    return vals.transpose(0, 1, 3, 2).reshape(g * 512, n)


def silu(v):
    return v / (1.0 + np.exp(-np.maximum(v, -700.0)))

def planes(y):
    n, m = y.shape
    v = y.astype(np.float32).astype(ml_dtypes.bfloat16).astype(np.float64).reshape(n // 32, 32, m)
    top = np.abs(v).max(1)
    byte = np.clip(np.where(top > 0, np.frexp(top)[1] - 1 + 127 - 7, 1), 1, 254)
    codes = (v * np.exp2(127.0 - byte)[:, None, :]).reshape(n, m).astype(np.float32).astype(ml_dtypes.float8_e4m3fn).view(np.uint8)
    words = codes.reshape(n // 512, 128, 4, m).transpose(0, 1, 3, 2)
    return np.ascontiguousarray(words), np.ascontiguousarray(byte.astype(np.uint8).reshape(n // 512, 16, m))


K, T, H = 512, 512, 512


def setup_inputs():
    n = np.random.standard_normal
    s = mx_kscale(K)[:, None]
    u = mx_kscale(H)
    packed_xT = pack_weight(n((K, T)) * s)
    packed_w2 = pack_fp4(n((H, H)) / np.sqrt(3 * H) / u[:, None])
    packed_w3 = pack_fp4(n((H, H)) / np.sqrt(3 * H) / u[:, None])
    packed_w4 = pack_fp4(n((H, H)) / np.sqrt(3 * H) / u[:, None])
    return {
        "x_words": packed_xT[0],
        "x_scales": packed_xT[1],
        "w1": (n((K, H)) / np.sqrt(K) / s * u).astype(np.float32),
        "w2_words": packed_w2[0],
        "w2_scales": packed_w2[1],
        "w3_words": packed_w3[0],
        "w3_scales": packed_w3[1],
        "w4_words": packed_w4[0],
        "w4_scales": packed_w4[1],
        "pos1": striped(np.random.permutation(T)),
        "pos2": striped(np.random.permutation(T)),
        "pos3": striped(np.random.permutation(T)),
        "pos4": striped(np.random.permutation(T)),
    }


def reference(x_words, x_scales, w1, w2_words, w2_scales, w3_words, w3_scales, w4_words, w4_scales, pos1, pos2, pos3, pos4):
    xq = unpack_weight(x_words, x_scales)
    h = silu(mxq(f64(w1), 0, "e4m3").T @ xq)
    g0 = h[:, unstriped(pos1)]
    g1 = h[:, unstriped(pos2)]
    g2 = h[:, unstriped(pos3)]
    g3 = h[:, unstriped(pos4)]
    z1 = (g0 + g1 + g2 + g3) / 4
    z2 = np.maximum(np.maximum(np.maximum(g0, g1), g2), g3)
    z3 = np.minimum(np.minimum(np.minimum(g0, g1), g2), g3)
    out_0 = unpack_fp4(w2_words, w2_scales).T @ mxq(z1, 0, "e4m3") + unpack_fp4(w3_words, w3_scales).T @ mxq(z2, 0, "e4m3") + unpack_fp4(w4_words, w4_scales).T @ mxq(z3, 0, "e4m3")
    return (out_0,) + planes(out_0)

@@ -1,0 +1,207 @@
+from contextlib import ExitStack
+
+import concourse.mybir as mybir
+from concourse.masks import make_identity
+
+F32 = mybir.dt.float32
+BF16 = mybir.dt.bfloat16
+I32 = mybir.dt.int32
+U32 = mybir.dt.uint32
+U16 = mybir.dt.uint16
+U8 = mybir.dt.uint8
+FP8X4 = mybir.dt.float8_e4m3fn_x4
+FP4X4 = mybir.dt.float4_e2m1fn_x4
+ACT = mybir.ActivationFunctionType
+ALU = mybir.AluOpType
+
+P = 128
+PACK = 4
+T = 512
+LISTS = 4
+HALF = 256
+BLK = 128
+FLOPS = 4 * 2 * 512 * 512 * 512
+
+
+def tile_picked_wpna_silu_lo_kernel(
+    tc, x_words, x_scales, w1, w2_words, w2_scales, w3_words, w3_scales, w4_words, w4_scales,
+    pos1, pos2, pos3, pos4, out_0, out_1, out_2,
+):
+    nc = tc.nc
+    with ExitStack() as ctx:
+        keep = ctx.enter_context(tc.tile_pool(name="keep", bufs=1))
+        psum = ctx.enter_context(tc.psum_pool(name="psum", bufs=1))
+
+        def sb(name, shape, dtype):
+            return keep.tile(shape, dtype, name=name, align_bytes=64)
+
+        def bank(index, name, shape):
+            return psum.tile(shape, F32, name=name, tag="bank%d" % index)
+
+        def load_scale_rows(queue, plane, rows):
+            for q in range(4):
+                queue.dma_start(out=plane[32 * q : 32 * q + 4, :].bitcast(I32), in_=rows[0, 4 * q : 4 * q + 4, :].bitcast(I32))
+
+        x_scale = sb("x_scale", [P, T], U8)
+        nc.vector.memset(x_scale[:].bitcast(I32), 0)
+        w_scale_raw = sb("w_scale_raw", [P, 3 * T], U8)
+        nc.vector.memset(w_scale_raw[:].bitcast(I32), 0)
+        load_scale_rows(nc.scalar, x_scale, x_scales)
+
+        w1_rows = w1.rearrange("(p j) c -> p j c", j=PACK)
+        w1_raw = []
+        for half in range(2):
+            raw = sb("w1_raw%d" % half, [P, PACK, HALF], F32)
+            nc.sync.dma_start(out=raw[:], in_=w1_rows[:, :, half * HALF : (half + 1) * HALF])
+            w1_raw.append(raw)
+        x_code = sb("x_code", [P, T], U32)
+        nc.sync.dma_start(out=x_code[:].bitcast(I32), in_=x_words[0].rearrange("p v r -> p (v r)").bitcast(I32))
+
+        offsets = [keep.tile([P, T // 16], U16, name="offsets%d" % d) for d in range(LISTS)]
+        lists = (pos1, pos2, pos3, pos4)
+        nc.sync.dma_start(offsets[0][:], lists[0])
+        w_word_raw = []
+        for s, words in enumerate((w2_words, w3_words, w4_words)):
+            raw = sb("w_word_raw%d" % s, [P, 2 * T], U8)
+            nc.sync.dma_start(out=raw[:].bitcast(I32), in_=words[0].bitcast(I32))
+            w_word_raw.append(raw)
+        for d in range(1, LISTS):
+            nc.sync.dma_start(offsets[d][:], lists[d])
+        for s, rows in enumerate((w2_scales, w3_scales, w4_scales)):
+            load_scale_rows(nc.sync, w_scale_raw[:, s * T : (s + 1) * T], rows)
+
+        ident = sb("ident", [P, P], F32)
+        make_identity(nc, ident[:])
+
+        w1_bf = sb("w1_bf", [P, PACK, P, PACK], BF16)
+        for half in range(2):
+            nc.vector.tensor_copy(
+                out=w1_bf[:, :, half * 64 : (half + 1) * 64, :].rearrange("p t m j -> p m j t"),
+                in_=w1_raw[half][:].rearrange("p j (m t) -> p m j t", t=PACK),
+            )
+        h = []
+        for t in range(PACK):
+            code = sb("w1_code%d" % t, [P, P], U32)
+            scale = sb("w1_scale%d" % t, [P, P], U8)
+            nc.vector.quantize_mx(out=code[:].bitcast(FP8X4), scales=scale[:], in_=w1_bf[:, t, :, :].rearrange("p m j -> p (m j)"))
+            pre = bank(t, "pre%d" % t, [P, T])
+            nc.tensor.matmul_mx(
+                out=pre[:], lhsT=code[:].bitcast(FP8X4), lhsT_scale=scale[:],
+                rhs=x_code[:].bitcast(FP8X4), rhs_scale=x_scale[:], start=True, stop=True,
+            )
+            plane = sb("h%d" % t, [P, T], F32)
+            nc.scalar.activation(out=plane[:], in_=pre[:], func=ACT.Silu)
+            h.append(plane)
+
+        w_word = []
+        for s in range(3):
+            dealt = sb("w_word%d" % s, [P, 2 * T], U8)
+            nc.vector.tensor_copy(
+                out=dealt[:].rearrange("p (t m b) -> p m t b", t=PACK, b=2),
+                in_=w_word_raw[s][:].rearrange("p (m t b) -> p m t b", t=PACK, b=2),
+            )
+            w_word.append(dealt)
+
+        mean_banks = ((4, 5), (0, 1))
+        rounded = []
+        z1_bf = []
+        for half in range(2):
+            gb = sb("rounded%d" % half, [P, LISTS, HALF * PACK], BF16)
+            sums = [bank(mean_banks[half][b], "sum%d_%d" % (half, b), [P, PACK, P]) for b in range(2)]
+            for d in range(LISTS):
+                g = sb("g%d_%d" % (half, d), [P, PACK, HALF], F32)
+                offs = offsets[d][:, half * 16 : (half + 1) * 16]
+                for t in range(PACK):
+                    nc.vector.tensor_copy(g[:, t, :], h[t][:].indirect(offs))
+                for b in range(2):
+                    for t in range(PACK):
+                        nc.tensor.matmul(
+                            sums[b][:, t, :], g[:, t, b * BLK : (b + 1) * BLK], ident[:],
+                            start=(d == 0 and t == 0), stop=(d == LISTS - 1 and t == PACK - 1), is_transpose=True,
+                        )
+                nc.scalar.copy(
+                    out=gb[:, d, :].rearrange("p (c i t) -> p c t i", i=4, t=PACK),
+                    in_=g[:].rearrange("p t (c i) -> p c t i", i=4),
+                )
+            back = bank(6 + half, "back%d" % half, [P, 2, HALF])
+            for b in range(2):
+                pairs = sb("pairs%d_%d" % (half, b), [P, 2 * P * 2], BF16)
+                nc.scalar.activation(
+                    out=pairs[:].rearrange("k (u p e) -> k u p e", u=2, e=2),
+                    in_=sums[b][:].rearrange("k (u e) p -> k u p e", e=2),
+                    func=ACT.Copy, scale=1.0 / LISTS,
+                )
+                for u in range(2):
+                    nc.tensor.transpose(back[:, u, b * BLK : (b + 1) * BLK], pairs[:].bitcast(F32)[:, u * P : (u + 1) * P], ident[:])
+            z1 = sb("z1_%d" % half, [P, HALF * PACK], BF16)
+            nc.scalar.copy(out=z1[:].bitcast(F32).rearrange("p (k u) -> p k u", u=2), in_=back[:].rearrange("p u k -> p k u"))
+            rounded.append(gb)
+            z1_bf.append(z1)
+
+        w_scale = sb("w_scale", [P, 3 * T], U8)
+        nc.vector.tensor_copy(
+            out=w_scale[:].rearrange("p (s t m) -> p s m t", s=3, t=PACK),
+            in_=w_scale_raw[:].rearrange("p (s m t) -> p s m t", s=3, t=PACK),
+        )
+
+        out_code = sb("out_code", [P, T], U32)
+        out_scale = sb("out_scale", [P, T], U8)
+        out_rows = out_0.rearrange("(p t) v -> p t v", t=PACK)
+        out_words = out_1[0].rearrange("p v r -> p (v r)").bitcast(I32)
+        out_banks = ((2, 3, 4, 5), (0, 1, 6, 7))
+        z1_code = None
+        z1_scale = None
+        for c in range(4):
+            half, b = divmod(c, 2)
+            cols = slice(c * BLK, (c + 1) * BLK)
+            part = slice(b * BLK * PACK, (b + 1) * BLK * PACK)
+            gb = rounded[half]
+            hi = sb("hi%d" % c, [P, 2, BLK * PACK], BF16)
+            lo = sb("lo%d" % c, [P, 2, BLK * PACK], BF16)
+            nc.vector.tensor_tensor(hi[:], gb[:, 0:2, part], gb[:, 2:4, part], ALU.max)
+            nc.vector.tensor_tensor(lo[:], gb[:, 0:2, part], gb[:, 2:4, part], ALU.min)
+            z23 = sb("z23_%d" % c, [P, 2 * BLK * PACK], BF16)
+            nc.vector.tensor_tensor(z23[:, 0 : BLK * PACK], hi[:, 0, :], hi[:, 1, :], ALU.max)
+            nc.vector.tensor_tensor(z23[:, BLK * PACK :], lo[:, 0, :], lo[:, 1, :], ALU.min)
+            if b == 0:
+                z1_code = sb("z1_code%d" % half, [P, HALF], U32)
+                z1_scale = sb("z1_scale%d" % half, [P, HALF], U8)
+                nc.vector.quantize_mx(out=z1_code[:].bitcast(FP8X4), scales=z1_scale[:], in_=z1_bf[half][:])
+            z23_code = sb("z23_code%d" % c, [P, 2 * BLK], U32)
+            z23_scale = sb("z23_scale%d" % c, [P, 2 * BLK], U8)
+            nc.vector.quantize_mx(out=z23_code[:].bitcast(FP8X4), scales=z23_scale[:], in_=z23[:])
+            moving = (
+                (z1_code[:, b * BLK : (b + 1) * BLK], z1_scale[:, b * BLK : (b + 1) * BLK]),
+                (z23_code[:, 0:BLK], z23_scale[:, 0:BLK]),
+                (z23_code[:, BLK:], z23_scale[:, BLK:]),
+            )
+            acc = [bank(out_banks[c % 2][t], "acc%d_%d" % (c, t), [P, BLK]) for t in range(PACK)]
+            for s in range(3):
+                for t in range(PACK):
+                    nc.tensor.matmul_mx(
+                        out=acc[t][:],
+                        lhsT=w_word[s][:, t * 2 * P : (t + 1) * 2 * P].bitcast(FP4X4),
+                        lhsT_scale=w_scale[:, s * T + t * P : s * T + (t + 1) * P],
+                        rhs=moving[s][0].bitcast(FP8X4), rhs_scale=moving[s][1],
+                        start=(s == 0), stop=(s == 2),
+                    )
+            res = sb("res%d" % c, [P, PACK, BLK], F32)
+            res_bf = sb("res_bf%d" % c, [P, BLK * PACK], BF16)
+            last = c == 3
+            for t in range(PACK):
+                if last and t % 2 == 1:
+                    nc.vector.tensor_copy(out=res[:, t, :], in_=acc[t][:])
+                else:
+                    nc.scalar.copy(out=res[:, t, :], in_=acc[t][:])
+            nc.sync.dma_start(out=out_rows[:, :, cols], in_=res[:])
+            dst = res_bf[:].rearrange("p (c i t) -> p c t i", i=4, t=PACK)
+            src = res[:].rearrange("p t (c i) -> p c t i", i=4)
+            if last:
+                nc.vector.tensor_copy(out=dst, in_=src)
+            else:
+                nc.scalar.copy(out=dst, in_=src)
+            nc.vector.quantize_mx(out=out_code[:, cols].bitcast(FP8X4), scales=out_scale[:, cols], in_=res_bf[:])
+            nc.sync.dma_start(out=out_words[:, cols], in_=out_code[:, cols].bitcast(I32))
+        for q in range(4):
+            queue = nc.sync if q % 2 == 0 else nc.scalar
+            queue.dma_start(out=out_2[0, 4 * q : 4 * q + 4, :].bitcast(I32), in_=out_scale[32 * q : 32 * q + 4, :].bitcast(I32))

@@ -45,71 +45,78 @@ def tile_picked_wpna_silu_lo_kernel(
         x_scale = sb("x_scale", [P, T], U8)
         nc.vector.memset(x_scale[:].bitcast(I32), 0)
         w_scale_raw = sb("w_scale_raw", [P, 3 * T], U8)
-        nc.vector.memset(w_scale_raw[:].bitcast(I32), 0)
-        load_scale_rows(nc.scalar, x_scale, x_scales)
+        nc.gpsimd.memset(w_scale_raw[:].bitcast(I32), 0)
+        load_scale_rows(nc.sync, x_scale, x_scales)
 
         w1_rows = w1.rearrange("(p j) c -> p j c", j=PACK)
         w1_raw = []
-        for half in range(2):
-            raw = sb("w1_raw%d" % half, [P, PACK, HALF], F32)
-            nc.sync.dma_start(out=raw[:], in_=w1_rows[:, :, half * HALF : (half + 1) * HALF])
+        w1_cuts = (0, 320, T)
+        for c0, c1 in zip(w1_cuts, w1_cuts[1:]):
+            raw = sb("w1_raw%d" % c0, [P, PACK, c1 - c0], F32)
+            nc.sync.dma_start(out=raw[:], in_=w1_rows[:, :, c0:c1])
             w1_raw.append(raw)
         x_code = sb("x_code", [P, T], U32)
         nc.sync.dma_start(out=x_code[:].bitcast(I32), in_=x_words[0].rearrange("p v r -> p (v r)").bitcast(I32))
 
         offsets = [keep.tile([P, T // 16], U16, name="offsets%d" % d) for d in range(LISTS)]
         lists = (pos1, pos2, pos3, pos4)
-        nc.sync.dma_start(offsets[0][:], lists[0])
+        for d in range(LISTS):
+            nc.sync.dma_start(offsets[d][:], lists[d])
         w_word_raw = []
         for s, words in enumerate((w2_words, w3_words, w4_words)):
             raw = sb("w_word_raw%d" % s, [P, 2 * T], U8)
             nc.sync.dma_start(out=raw[:].bitcast(I32), in_=words[0].bitcast(I32))
             w_word_raw.append(raw)
-        for d in range(1, LISTS):
-            nc.sync.dma_start(offsets[d][:], lists[d])
         for s, rows in enumerate((w2_scales, w3_scales, w4_scales)):
             load_scale_rows(nc.sync, w_scale_raw[:, s * T : (s + 1) * T], rows)
 
         ident = sb("ident", [P, P], F32)
         make_identity(nc, ident[:])
 
-        w1_bf = sb("w1_bf", [P, PACK, P, PACK], BF16)
-        for half in range(2):
+        w1_bf = keep.tile([P, PACK, P, PACK], BF16, name="w1_bf", tag="w1_bf", align_bytes=64)
+        for raw, c0, c1 in zip(w1_raw, w1_cuts, w1_cuts[1:]):
             nc.vector.tensor_copy(
-                out=w1_bf[:, :, half * 64 : (half + 1) * 64, :].rearrange("p t m j -> p m j t"),
-                in_=w1_raw[half][:].rearrange("p j (m t) -> p m j t", t=PACK),
+                out=w1_bf[:, :, c0 // PACK : c1 // PACK, :].rearrange("p t m j -> p m j t"),
+                in_=raw[:].rearrange("p j (m t) -> p m j t", t=PACK),
             )
         h = []
         for t in range(PACK):
             code = sb("w1_code%d" % t, [P, P], U32)
             scale = sb("w1_scale%d" % t, [P, P], U8)
             nc.vector.quantize_mx(out=code[:].bitcast(FP8X4), scales=scale[:], in_=w1_bf[:, t, :, :].rearrange("p m j -> p (m j)"))
-            pre = bank(t, "pre%d" % t, [P, T])
-            nc.tensor.matmul_mx(
-                out=pre[:], lhsT=code[:].bitcast(FP8X4), lhsT_scale=scale[:],
-                rhs=x_code[:].bitcast(FP8X4), rhs_scale=x_scale[:], start=True, stop=True,
-            )
             plane = sb("h%d" % t, [P, T], F32)
-            nc.scalar.activation(out=plane[:], in_=pre[:], func=ACT.Silu)
+            pieces = ((7, 0, HALF), (0, HALF, T)) if t == 0 else ((t, 0, T),)
+            for index, v0, v1 in pieces:
+                pre = bank(index, "pre%d_%d" % (t, v0), [P, v1 - v0])
+                nc.tensor.matmul_mx(
+                    out=pre[:], lhsT=code[:].bitcast(FP8X4), lhsT_scale=scale[:],
+                    rhs=x_code[:, v0:v1].bitcast(FP8X4), rhs_scale=x_scale[:, v0:v1], start=True, stop=True,
+                )
+                nc.scalar.activation(out=plane[:, v0:v1], in_=pre[:], func=ACT.Silu)
             h.append(plane)
 
-        w_word = []
+        dealt = keep.tile([P, 3 * 2 * T], U8, name="dealt", tag="w1_bf", align_bytes=64)
+        w_word = [dealt[:, s * 2 * T : (s + 1) * 2 * T] for s in range(3)]
         for s in range(3):
-            dealt = sb("w_word%d" % s, [P, 2 * T], U8)
-            nc.vector.tensor_copy(
-                out=dealt[:].rearrange("p (t m b) -> p m t b", t=PACK, b=2),
-                in_=w_word_raw[s][:].rearrange("p (m t b) -> p m t b", t=PACK, b=2),
+            nc.gpsimd.tensor_copy(
+                out=w_word[s].rearrange("p (t m b) -> p t m b", t=PACK, b=2),
+                in_=w_word_raw[s][:].rearrange("p (m t b) -> p t m b", t=PACK, b=2),
             )
-            w_word.append(dealt)
+        w_scale = sb("w_scale", [P, 3 * T], U8)
+        nc.gpsimd.tensor_copy(
+            out=w_scale[:].rearrange("p (s t m) -> p s t m", s=3, t=PACK),
+            in_=w_scale_raw[:].rearrange("p (s m t) -> p s t m", s=3, t=PACK),
+        )
 
-        mean_banks = ((4, 5), (0, 1))
+        mean_banks = ((4, 5), (6, 7))
+        back_banks = ((6, 7), (0, 1))
         rounded = []
         z1_bf = []
         for half in range(2):
             gb = sb("rounded%d" % half, [P, LISTS, HALF * PACK], BF16)
             sums = [bank(mean_banks[half][b], "sum%d_%d" % (half, b), [P, PACK, P]) for b in range(2)]
             for d in range(LISTS):
-                g = sb("g%d_%d" % (half, d), [P, PACK, HALF], F32)
+                g = keep.tile([P, PACK, HALF], F32, name="g%d_%d" % (half, d), tag="g%d" % d, align_bytes=64)
                 offs = offsets[d][:, half * 16 : (half + 1) * 16]
                 for t in range(PACK):
                     nc.vector.tensor_copy(g[:, t, :], h[t][:].indirect(offs))
@@ -123,8 +130,9 @@ def tile_picked_wpna_silu_lo_kernel(
                     out=gb[:, d, :].rearrange("p (c i t) -> p c t i", i=4, t=PACK),
                     in_=g[:].rearrange("p t (c i) -> p c t i", i=4),
                 )
-            back = bank(6 + half, "back%d" % half, [P, 2, HALF])
+            z1 = sb("z1_%d" % half, [P, HALF * PACK], BF16)
             for b in range(2):
+                back = bank(back_banks[half][b], "back%d_%d" % (half, b), [P, 2, BLK])
                 pairs = sb("pairs%d_%d" % (half, b), [P, 2 * P * 2], BF16)
                 nc.scalar.activation(
                     out=pairs[:].rearrange("k (u p e) -> k u p e", u=2, e=2),
@@ -132,49 +140,53 @@ def tile_picked_wpna_silu_lo_kernel(
                     func=ACT.Copy, scale=1.0 / LISTS,
                 )
                 for u in range(2):
-                    nc.tensor.transpose(back[:, u, b * BLK : (b + 1) * BLK], pairs[:].bitcast(F32)[:, u * P : (u + 1) * P], ident[:])
-            z1 = sb("z1_%d" % half, [P, HALF * PACK], BF16)
-            nc.scalar.copy(out=z1[:].bitcast(F32).rearrange("p (k u) -> p k u", u=2), in_=back[:].rearrange("p u k -> p k u"))
+                    nc.tensor.transpose(back[:, u, :], pairs[:].bitcast(F32)[:, u * P : (u + 1) * P], ident[:])
+                nc.scalar.copy(
+                    out=z1[:].bitcast(F32)[:, b * 2 * BLK : (b + 1) * 2 * BLK].rearrange("p (k u) -> p k u", u=2),
+                    in_=back[:].rearrange("p u k -> p k u"),
+                )
             rounded.append(gb)
             z1_bf.append(z1)
 
-        w_scale = sb("w_scale", [P, 3 * T], U8)
-        nc.vector.tensor_copy(
-            out=w_scale[:].rearrange("p (s t m) -> p s m t", s=3, t=PACK),
-            in_=w_scale_raw[:].rearrange("p (s m t) -> p s m t", s=3, t=PACK),
-        )
 
         out_code = sb("out_code", [P, T], U32)
         out_scale = sb("out_scale", [P, T], U8)
         out_rows = out_0.rearrange("(p t) v -> p t v", t=PACK)
         out_words = out_1[0].rearrange("p v r -> p (v r)").bitcast(I32)
         out_banks = ((2, 3, 4, 5), (0, 1, 6, 7))
-        z1_code = None
-        z1_scale = None
-        for c in range(4):
+        W = BLK * PACK
+        moving = {}
+        res_bf = {}
+        result = {}
+        level = {}
+
+        def first_level(c, op, name):
             half, b = divmod(c, 2)
-            cols = slice(c * BLK, (c + 1) * BLK)
-            part = slice(b * BLK * PACK, (b + 1) * BLK * PACK)
-            gb = rounded[half]
-            hi = sb("hi%d" % c, [P, 2, BLK * PACK], BF16)
-            lo = sb("lo%d" % c, [P, 2, BLK * PACK], BF16)
-            nc.vector.tensor_tensor(hi[:], gb[:, 0:2, part], gb[:, 2:4, part], ALU.max)
-            nc.vector.tensor_tensor(lo[:], gb[:, 0:2, part], gb[:, 2:4, part], ALU.min)
-            z23 = sb("z23_%d" % c, [P, 2 * BLK * PACK], BF16)
-            nc.vector.tensor_tensor(z23[:, 0 : BLK * PACK], hi[:, 0, :], hi[:, 1, :], ALU.max)
-            nc.vector.tensor_tensor(z23[:, BLK * PACK :], lo[:, 0, :], lo[:, 1, :], ALU.min)
-            if b == 0:
-                z1_code = sb("z1_code%d" % half, [P, HALF], U32)
-                z1_scale = sb("z1_scale%d" % half, [P, HALF], U8)
-                nc.vector.quantize_mx(out=z1_code[:].bitcast(FP8X4), scales=z1_scale[:], in_=z1_bf[half][:])
-            z23_code = sb("z23_code%d" % c, [P, 2 * BLK], U32)
-            z23_scale = sb("z23_scale%d" % c, [P, 2 * BLK], U8)
-            nc.vector.quantize_mx(out=z23_code[:].bitcast(FP8X4), scales=z23_scale[:], in_=z23[:])
-            moving = (
-                (z1_code[:, b * BLK : (b + 1) * BLK], z1_scale[:, b * BLK : (b + 1) * BLK]),
-                (z23_code[:, 0:BLK], z23_scale[:, 0:BLK]),
-                (z23_code[:, BLK:], z23_scale[:, BLK:]),
-            )
+            part = slice(b * W, (b + 1) * W)
+            if c not in level:
+                level[c] = keep.tile([P, 2, 2, W], BF16, name="level%d" % c, tag="g%d" % (2 + c % 2), align_bytes=64)
+            pair = level[c][:, 0 if name == "hi" else 1, :, :]
+            nc.vector.tensor_tensor(pair, rounded[half][:, 0:2, part], rounded[half][:, 2:4, part], op)
+            return pair
+
+        def quantise(name, values, keys):
+            width = BLK * len(keys)
+            code = sb(name + "_code", [P, width], U32)
+            scale = sb(name + "_scale", [P, width], U8)
+            nc.vector.quantize_mx(out=code[:].bitcast(FP8X4), scales=scale[:], in_=values)
+            for i, key in enumerate(keys):
+                moving[key] = (code[:, i * BLK : (i + 1) * BLK], scale[:, i * BLK : (i + 1) * BLK])
+
+        def extremes(c):
+            hi = first_level(c, ALU.max, "hi")
+            lo = first_level(c, ALU.min, "lo")
+            z23 = sb("z23_%d" % c, [P, 2 * W], BF16)
+            nc.vector.tensor_tensor(z23[:, 0:W], hi[:, 0, :], hi[:, 1, :], ALU.max)
+            nc.vector.tensor_tensor(z23[:, W:], lo[:, 0, :], lo[:, 1, :], ALU.min)
+            return z23
+
+        def product(c):
+            last = c == 3
             acc = [bank(out_banks[c % 2][t], "acc%d_%d" % (c, t), [P, BLK]) for t in range(PACK)]
             for s in range(3):
                 for t in range(PACK):
@@ -182,26 +194,54 @@ def tile_picked_wpna_silu_lo_kernel(
                         out=acc[t][:],
                         lhsT=w_word[s][:, t * 2 * P : (t + 1) * 2 * P].bitcast(FP4X4),
                         lhsT_scale=w_scale[:, s * T + t * P : s * T + (t + 1) * P],
-                        rhs=moving[s][0].bitcast(FP8X4), rhs_scale=moving[s][1],
+                        rhs=moving[c, s][0].bitcast(FP8X4), rhs_scale=moving[c, s][1],
                         start=(s == 0), stop=(s == 2),
                     )
             res = sb("res%d" % c, [P, PACK, BLK], F32)
-            res_bf = sb("res_bf%d" % c, [P, BLK * PACK], BF16)
-            last = c == 3
+            res_bf[c] = sb("res_bf%d" % c, [P, W], BF16)
             for t in range(PACK):
                 if last and t % 2 == 1:
                     nc.vector.tensor_copy(out=res[:, t, :], in_=acc[t][:])
                 else:
                     nc.scalar.copy(out=res[:, t, :], in_=acc[t][:])
-            nc.sync.dma_start(out=out_rows[:, :, cols], in_=res[:])
-            dst = res_bf[:].rearrange("p (c i t) -> p c t i", i=4, t=PACK)
-            src = res[:].rearrange("p t (c i) -> p c t i", i=4)
-            if last:
-                nc.vector.tensor_copy(out=dst, in_=src)
-            else:
-                nc.scalar.copy(out=dst, in_=src)
-            nc.vector.quantize_mx(out=out_code[:, cols].bitcast(FP8X4), scales=out_scale[:, cols], in_=res_bf[:])
+            queue = nc.scalar if last else nc.sync
+            queue.dma_start(out=out_rows[:, :, c * BLK : (c + 1) * BLK], in_=res[:])
+            result[c] = res
+            if c < 2:
+                weave(c, nc.scalar.copy)
+
+        def weave(c, copy):
+            copy(
+                out=res_bf[c][:].rearrange("p (c i t) -> p c t i", i=4, t=PACK),
+                in_=result[c][:].rearrange("p t (c i) -> p c t i", i=4),
+            )
+
+        def planes(c):
+            cols = slice(c * BLK, (c + 1) * BLK)
+            nc.vector.quantize_mx(out=out_code[:, cols].bitcast(FP8X4), scales=out_scale[:, cols], in_=res_bf[c][:])
             nc.sync.dma_start(out=out_words[:, cols], in_=out_code[:, cols].bitcast(I32))
+
+        for c in range(3):
+            if c % 2 == 0:
+                quantise("z1_%d" % c, z1_bf[c // 2][:], ((c, 0), (c + 1, 0)))
+            z23 = extremes(c)
+            quantise("z23_%d" % c, z23[:], ((c, 1), (c, 2)))
+            product(c)
+        hi = first_level(3, ALU.max, "hi")
+        lo = first_level(3, ALU.min, "lo")
+        z2 = sb("z2_last", [P, W], BF16)
+        nc.vector.tensor_tensor(z2[:], hi[:, 0, :], hi[:, 1, :], ALU.max)
+        z3 = sb("z3_last", [P, W], BF16)
+        nc.vector.tensor_tensor(z3[:], lo[:, 0, :], lo[:, 1, :], ALU.min)
+        quantise("z2_last", z2[:], ((3, 1),))
+        quantise("z3_last", z3[:], ((3, 2),))
+        planes(0)
+        planes(1)
+        weave(2, nc.vector.tensor_copy)
+        planes(2)
+        product(3)
+        weave(3, nc.vector.tensor_copy)
+        planes(3)
         for q in range(4):
             queue = nc.sync if q % 2 == 0 else nc.scalar
             queue.dma_start(out=out_2[0, 4 * q : 4 * q + 4, :].bitcast(I32), in_=out_scale[32 * q : 32 * q + 4, :].bitcast(I32))

@@ -79,12 +79,11 @@ def tile_picked_wpna_silu_lo_kernel(
                 out=w1_bf[:, :, c0 // PACK : c1 // PACK, :].rearrange("p t m j -> p m j t"),
                 in_=raw[:].rearrange("p j (m t) -> p m j t", t=PACK),
             )
-        h = []
+        h = sb("h", [P, PACK * T], F32)
         for t in range(PACK):
             code = sb("w1_code%d" % t, [P, P], U32)
             scale = sb("w1_scale%d" % t, [P, P], U8)
             nc.vector.quantize_mx(out=code[:].bitcast(FP8X4), scales=scale[:], in_=w1_bf[:, t, :, :].rearrange("p m j -> p (m j)"))
-            plane = sb("h%d" % t, [P, T], F32)
             pieces = ((7, 0, HALF), (0, HALF, T)) if t == 0 else ((t, 0, T),)
             for index, v0, v1 in pieces:
                 pre = bank(index, "pre%d_%d" % (t, v0), [P, v1 - v0])
@@ -92,8 +91,7 @@ def tile_picked_wpna_silu_lo_kernel(
                     out=pre[:], lhsT=code[:].bitcast(FP8X4), lhsT_scale=scale[:],
                     rhs=x_code[:, v0:v1].bitcast(FP8X4), rhs_scale=x_scale[:, v0:v1], start=True, stop=True,
                 )
-                nc.scalar.activation(out=plane[:, v0:v1], in_=pre[:], func=ACT.Silu)
-            h.append(plane)
+                nc.scalar.activation(out=h[:, t * T + v0 : t * T + v1], in_=pre[:], func=ACT.Silu)
 
         dealt = keep.tile([P, 3 * 2 * T], U8, name="dealt", tag="w1_bf", align_bytes=64)
         w_word = [dealt[:, s * 2 * T : (s + 1) * 2 * T] for s in range(3)]
@@ -108,52 +106,68 @@ def tile_picked_wpna_silu_lo_kernel(
             in_=w_scale_raw[:].rearrange("p (s m t) -> p s t m", s=3, t=PACK),
         )
 
-        mean_banks = ((4, 5), (6, 7))
-        back_banks = ((6, 7), (0, 1))
-        rounded = []
-        z1_bf = []
-        for half in range(2):
-            gb = sb("rounded%d" % half, [P, LISTS, HALF * PACK], BF16)
-            sums = [bank(mean_banks[half][b], "sum%d_%d" % (half, b), [P, PACK, P]) for b in range(2)]
-            for d in range(LISTS):
-                g = keep.tile([P, PACK, HALF], F32, name="g%d_%d" % (half, d), tag="g%d" % d, align_bytes=64)
-                offs = offsets[d][:, half * 16 : (half + 1) * 16]
-                for t in range(PACK):
-                    nc.vector.tensor_copy(g[:, t, :], h[t][:].indirect(offs))
+        mean_banks = ((4, 5), (0, 1))
+        back_banks = ((6, 7), (2, 3))
+        rounded = [sb("rounded%d" % half, [P, LISTS, HALF * PACK], BF16) for half in range(2)]
+        z1_bf = [sb("z1_%d" % half, [P, HALF * PACK], BF16) for half in range(2)]
+        sums = {}
+        backs = {}
+
+        def fetch(half, d):
+            if d == 0:
+                sums[half] = [bank(mean_banks[half][b], "sum%d_%d" % (half, b), [P, PACK, P]) for b in range(2)]
+            g = keep.tile([P, PACK, HALF], F32, name="g%d_%d" % (half, d), tag="g%d_%d" % (half, d), align_bytes=64)
+            offs = offsets[d][:, half * 16 : (half + 1) * 16]
+            for t in range(PACK):
+                early = half == 0 and (d == 0 or (d == 1 and t == 0))
+                end = (t + 1) * T if early else PACK * T
+                nc.vector.tensor_copy(g[:, t, :], h[:, t * T : end].indirect(offs))
                 for b in range(2):
-                    for t in range(PACK):
-                        nc.tensor.matmul(
-                            sums[b][:, t, :], g[:, t, b * BLK : (b + 1) * BLK], ident[:],
-                            start=(d == 0 and t == 0), stop=(d == LISTS - 1 and t == PACK - 1), is_transpose=True,
-                        )
-                nc.scalar.copy(
-                    out=gb[:, d, :].rearrange("p (c i t) -> p c t i", i=4, t=PACK),
-                    in_=g[:].rearrange("p t (c i) -> p c t i", i=4),
-                )
-            z1 = sb("z1_%d" % half, [P, HALF * PACK], BF16)
+                    nc.tensor.matmul(
+                        sums[half][b][:, t, :], g[:, t, b * BLK : (b + 1) * BLK], ident[:],
+                        start=(d == 0 and t == 0), stop=(d == LISTS - 1 and t == PACK - 1), is_transpose=True,
+                    )
+            return g
+
+        def round_list(half, d, g):
+            nc.scalar.copy(
+                out=rounded[half][:, d, :].rearrange("p (c i t) -> p c t i", i=4, t=PACK),
+                in_=g[:].rearrange("p t (c i) -> p c t i", i=4),
+            )
+
+        def mean_turn(half):
             for b in range(2):
-                back = bank(back_banks[half][b], "back%d_%d" % (half, b), [P, 2, BLK])
+                backs[half, b] = bank(back_banks[half][b], "back%d_%d" % (half, b), [P, 2, BLK])
                 pairs = sb("pairs%d_%d" % (half, b), [P, 2 * P * 2], BF16)
                 nc.scalar.activation(
                     out=pairs[:].rearrange("k (u p e) -> k u p e", u=2, e=2),
-                    in_=sums[b][:].rearrange("k (u e) p -> k u p e", e=2),
+                    in_=sums[half][b][:].rearrange("k (u e) p -> k u p e", e=2),
                     func=ACT.Copy, scale=1.0 / LISTS,
                 )
                 for u in range(2):
-                    nc.tensor.transpose(back[:, u, :], pairs[:].bitcast(F32)[:, u * P : (u + 1) * P], ident[:])
-                nc.scalar.copy(
-                    out=z1[:].bitcast(F32)[:, b * 2 * BLK : (b + 1) * 2 * BLK].rearrange("p (k u) -> p k u", u=2),
-                    in_=back[:].rearrange("p u k -> p k u"),
-                )
-            rounded.append(gb)
-            z1_bf.append(z1)
+                    nc.tensor.transpose(backs[half, b][:, u, :], pairs[:].bitcast(F32)[:, u * P : (u + 1) * P], ident[:])
 
+        def mean_out(half):
+            for b in range(2):
+                nc.scalar.copy(
+                    out=z1_bf[half][:].bitcast(F32)[:, b * 2 * BLK : (b + 1) * 2 * BLK].rearrange("p (k u) -> p k u", u=2),
+                    in_=backs[half, b][:].rearrange("p u k -> p k u"),
+                )
+
+        for half in range(2):
+            for d in range(LISTS):
+                g = fetch(half, d)
+                if (half, d) == (1, LISTS - 1):
+                    mean_out(0)
+                round_list(half, d, g)
+            mean_turn(half)
+        mean_out(1)
 
         out_code = sb("out_code", [P, T], U32)
         out_scale = sb("out_scale", [P, T], U8)
         out_rows = out_0.rearrange("(p t) v -> p t v", t=PACK)
         out_words = out_1[0].rearrange("p v r -> p (v r)").bitcast(I32)
-        out_banks = ((2, 3, 4, 5), (0, 1, 6, 7))
+        out_banks = ((4, 5, 6, 7), (0, 1, 2, 3))
         W = BLK * PACK
         moving = {}
         res_bf = {}
@@ -164,7 +178,7 @@ def tile_picked_wpna_silu_lo_kernel(
             half, b = divmod(c, 2)
             part = slice(b * W, (b + 1) * W)
             if c not in level:
-                level[c] = keep.tile([P, 2, 2, W], BF16, name="level%d" % c, tag="g%d" % (2 + c % 2), align_bytes=64)
+                level[c] = keep.tile([P, 2, 2, W], BF16, name="level%d" % c, tag="g1_%d" % (2 + c % 2), align_bytes=64)
             pair = level[c][:, 0 if name == "hi" else 1, :, :]
             nc.vector.tensor_tensor(pair, rounded[half][:, 0:2, part], rounded[half][:, 2:4, part], op)
             return pair

from contextlib import ExitStack

import concourse.mybir as mybir
from concourse.masks import make_identity

F32 = mybir.dt.float32
BF16 = mybir.dt.bfloat16
I32 = mybir.dt.int32
U32 = mybir.dt.uint32
U16 = mybir.dt.uint16
U8 = mybir.dt.uint8
FP8X4 = mybir.dt.float8_e4m3fn_x4
FP4X4 = mybir.dt.float4_e2m1fn_x4
ACT = mybir.ActivationFunctionType
ALU = mybir.AluOpType

P = 128
PACK = 4
T = 512
LISTS = 4
HALF = 256
BLK = 128
FLOPS = 4 * 2 * 512 * 512 * 512


def tile_picked_wpna_silu_lo_kernel(
    tc, x_words, x_scales, w1, w2_words, w2_scales, w3_words, w3_scales, w4_words, w4_scales,
    pos1, pos2, pos3, pos4, out_0, out_1, out_2,
):
    nc = tc.nc
    with ExitStack() as ctx:
        keep = ctx.enter_context(tc.tile_pool(name="keep", bufs=1))
        psum = ctx.enter_context(tc.psum_pool(name="psum", bufs=1))

        def sb(name, shape, dtype):
            return keep.tile(shape, dtype, name=name, align_bytes=64)

        def bank(index, name, shape):
            return psum.tile(shape, F32, name=name, tag="bank%d" % index)

        def load_scale_rows(queue, plane, rows):
            for q in range(4):
                queue.dma_start(out=plane[32 * q : 32 * q + 4, :].bitcast(I32), in_=rows[0, 4 * q : 4 * q + 4, :].bitcast(I32))

        x_scale = sb("x_scale", [P, T], U8)
        nc.vector.memset(x_scale[:].bitcast(I32), 0)
        w_scale_raw = sb("w_scale_raw", [P, 3 * T], U8)
        nc.gpsimd.memset(w_scale_raw[:].bitcast(I32), 0)
        load_scale_rows(nc.sync, x_scale, x_scales)

        w1_rows = w1.rearrange("(p j) c -> p j c", j=PACK)
        w1_raw = []
        w1_cuts = (0, 320, T)
        for c0, c1 in zip(w1_cuts, w1_cuts[1:]):
            raw = sb("w1_raw%d" % c0, [P, PACK, c1 - c0], F32)
            nc.sync.dma_start(out=raw[:], in_=w1_rows[:, :, c0:c1])
            w1_raw.append(raw)
        x_code = sb("x_code", [P, T], U32)
        nc.sync.dma_start(out=x_code[:].bitcast(I32), in_=x_words[0].rearrange("p v r -> p (v r)").bitcast(I32))

        offsets = [keep.tile([P, T // 16], U16, name="offsets%d" % d) for d in range(LISTS)]
        lists = (pos1, pos2, pos3, pos4)
        for d in range(LISTS):
            nc.sync.dma_start(offsets[d][:], lists[d])
        w_word_raw = []
        for s, words in enumerate((w2_words, w3_words, w4_words)):
            raw = sb("w_word_raw%d" % s, [P, 2 * T], U8)
            nc.sync.dma_start(out=raw[:].bitcast(I32), in_=words[0].bitcast(I32))
            w_word_raw.append(raw)
        for s, rows in enumerate((w2_scales, w3_scales, w4_scales)):
            load_scale_rows(nc.sync, w_scale_raw[:, s * T : (s + 1) * T], rows)

        ident = sb("ident", [P, P], F32)
        make_identity(nc, ident[:])

        w1_bf = keep.tile([P, PACK, P, PACK], BF16, name="w1_bf", tag="w1_bf", align_bytes=64)
        for raw, c0, c1 in zip(w1_raw, w1_cuts, w1_cuts[1:]):
            nc.vector.tensor_copy(
                out=w1_bf[:, :, c0 // PACK : c1 // PACK, :].rearrange("p t m j -> p m j t"),
                in_=raw[:].rearrange("p j (m t) -> p m j t", t=PACK),
            )
        h = sb("h", [P, PACK * T], F32)
        for t in range(PACK):
            code = sb("w1_code%d" % t, [P, P], U32)
            scale = sb("w1_scale%d" % t, [P, P], U8)
            nc.vector.quantize_mx(out=code[:].bitcast(FP8X4), scales=scale[:], in_=w1_bf[:, t, :, :].rearrange("p m j -> p (m j)"))
            pieces = ((7, 0, HALF), (0, HALF, T)) if t == 0 else ((t, 0, T),)
            for index, v0, v1 in pieces:
                pre = bank(index, "pre%d_%d" % (t, v0), [P, v1 - v0])
                nc.tensor.matmul_mx(
                    out=pre[:], lhsT=code[:].bitcast(FP8X4), lhsT_scale=scale[:],
                    rhs=x_code[:, v0:v1].bitcast(FP8X4), rhs_scale=x_scale[:, v0:v1], start=True, stop=True,
                )
                nc.scalar.activation(out=h[:, t * T + v0 : t * T + v1], in_=pre[:], func=ACT.Silu)

        dealt = keep.tile([P, 3 * 2 * T], U8, name="dealt", tag="w1_bf", align_bytes=64)
        w_word = [dealt[:, s * 2 * T : (s + 1) * 2 * T] for s in range(3)]
        for s in range(3):
            nc.gpsimd.tensor_copy(
                out=w_word[s].rearrange("p (t m b) -> p t m b", t=PACK, b=2),
                in_=w_word_raw[s][:].rearrange("p (m t b) -> p t m b", t=PACK, b=2),
            )
        w_scale = sb("w_scale", [P, 3 * T], U8)
        nc.gpsimd.tensor_copy(
            out=w_scale[:].rearrange("p (s t m) -> p s t m", s=3, t=PACK),
            in_=w_scale_raw[:].rearrange("p (s m t) -> p s t m", s=3, t=PACK),
        )

        mean_banks = ((4, 5), (0, 1))
        back_banks = ((6, 7), (2, 3))
        rounded = [sb("rounded%d" % half, [P, LISTS, HALF * PACK], BF16) for half in range(2)]
        z1_bf = [sb("z1_%d" % half, [P, HALF * PACK], BF16) for half in range(2)]
        sums = {}
        backs = {}

        def fetch(half, d):
            if d == 0:
                sums[half] = [bank(mean_banks[half][b], "sum%d_%d" % (half, b), [P, PACK, P]) for b in range(2)]
            g = keep.tile([P, PACK, HALF], F32, name="g%d_%d" % (half, d), tag="g%d_%d" % (half, d), align_bytes=64)
            offs = offsets[d][:, half * 16 : (half + 1) * 16]
            for t in range(PACK):
                early = half == 0 and (d == 0 or (d == 1 and t == 0))
                end = (t + 1) * T if early else PACK * T
                nc.vector.tensor_copy(g[:, t, :], h[:, t * T : end].indirect(offs))
                for b in range(2):
                    nc.tensor.matmul(
                        sums[half][b][:, t, :], g[:, t, b * BLK : (b + 1) * BLK], ident[:],
                        start=(d == 0 and t == 0), stop=(d == LISTS - 1 and t == PACK - 1), is_transpose=True,
                    )
            return g

        def round_list(half, d, g):
            nc.scalar.copy(
                out=rounded[half][:, d, :].rearrange("p (c i t) -> p c t i", i=4, t=PACK),
                in_=g[:].rearrange("p t (c i) -> p c t i", i=4),
            )

        def mean_turn(half):
            for b in range(2):
                backs[half, b] = bank(back_banks[half][b], "back%d_%d" % (half, b), [P, 2, BLK])
                pairs = sb("pairs%d_%d" % (half, b), [P, 2 * P * 2], BF16)
                nc.scalar.activation(
                    out=pairs[:].rearrange("k (u p e) -> k u p e", u=2, e=2),
                    in_=sums[half][b][:].rearrange("k (u e) p -> k u p e", e=2),
                    func=ACT.Copy, scale=1.0 / LISTS,
                )
                for u in range(2):
                    nc.tensor.transpose(backs[half, b][:, u, :], pairs[:].bitcast(F32)[:, u * P : (u + 1) * P], ident[:])

        def mean_out(half):
            for b in range(2):
                nc.scalar.copy(
                    out=z1_bf[half][:].bitcast(F32)[:, b * 2 * BLK : (b + 1) * 2 * BLK].rearrange("p (k u) -> p k u", u=2),
                    in_=backs[half, b][:].rearrange("p u k -> p k u"),
                )

        for half in range(2):
            for d in range(LISTS):
                g = fetch(half, d)
                if (half, d) == (1, LISTS - 1):
                    mean_out(0)
                round_list(half, d, g)
            mean_turn(half)
        mean_out(1)

        out_code = sb("out_code", [P, T], U32)
        out_scale = sb("out_scale", [P, T], U8)
        out_rows = out_0.rearrange("(p t) v -> p t v", t=PACK)
        out_words = out_1[0].rearrange("p v r -> p (v r)").bitcast(I32)
        out_banks = ((4, 5, 6, 7), (0, 1, 2, 3))
        W = BLK * PACK
        moving = {}
        res_bf = {}
        result = {}
        level = {}

        def first_level(c, op, name):
            half, b = divmod(c, 2)
            part = slice(b * W, (b + 1) * W)
            if c not in level:
                level[c] = keep.tile([P, 2, 2, W], BF16, name="level%d" % c, tag="g1_%d" % (2 + c % 2), align_bytes=64)
            pair = level[c][:, 0 if name == "hi" else 1, :, :]
            nc.vector.tensor_tensor(pair, rounded[half][:, 0:2, part], rounded[half][:, 2:4, part], op)
            return pair

        def quantise(name, values, keys):
            width = BLK * len(keys)
            code = sb(name + "_code", [P, width], U32)
            scale = sb(name + "_scale", [P, width], U8)
            nc.vector.quantize_mx(out=code[:].bitcast(FP8X4), scales=scale[:], in_=values)
            for i, key in enumerate(keys):
                moving[key] = (code[:, i * BLK : (i + 1) * BLK], scale[:, i * BLK : (i + 1) * BLK])

        def extremes(c):
            hi = first_level(c, ALU.max, "hi")
            lo = first_level(c, ALU.min, "lo")
            z23 = sb("z23_%d" % c, [P, 2 * W], BF16)
            nc.vector.tensor_tensor(z23[:, 0:W], hi[:, 0, :], hi[:, 1, :], ALU.max)
            nc.vector.tensor_tensor(z23[:, W:], lo[:, 0, :], lo[:, 1, :], ALU.min)
            return z23

        def product(c):
            last = c == 3
            acc = [bank(out_banks[c % 2][t], "acc%d_%d" % (c, t), [P, BLK]) for t in range(PACK)]
            for s in range(3):
                for t in range(PACK):
                    nc.tensor.matmul_mx(
                        out=acc[t][:],
                        lhsT=w_word[s][:, t * 2 * P : (t + 1) * 2 * P].bitcast(FP4X4),
                        lhsT_scale=w_scale[:, s * T + t * P : s * T + (t + 1) * P],
                        rhs=moving[c, s][0].bitcast(FP8X4), rhs_scale=moving[c, s][1],
                        start=(s == 0), stop=(s == 2),
                    )
            res = sb("res%d" % c, [P, PACK, BLK], F32)
            res_bf[c] = sb("res_bf%d" % c, [P, W], BF16)
            for t in range(PACK):
                if last and t % 2 == 1:
                    nc.vector.tensor_copy(out=res[:, t, :], in_=acc[t][:])
                else:
                    nc.scalar.copy(out=res[:, t, :], in_=acc[t][:])
            queue = nc.scalar if last else nc.sync
            queue.dma_start(out=out_rows[:, :, c * BLK : (c + 1) * BLK], in_=res[:])
            result[c] = res
            if c < 2:
                weave(c, nc.scalar.copy)

        def weave(c, copy):
            copy(
                out=res_bf[c][:].rearrange("p (c i t) -> p c t i", i=4, t=PACK),
                in_=result[c][:].rearrange("p t (c i) -> p c t i", i=4),
            )

        def planes(c):
            cols = slice(c * BLK, (c + 1) * BLK)
            nc.vector.quantize_mx(out=out_code[:, cols].bitcast(FP8X4), scales=out_scale[:, cols], in_=res_bf[c][:])
            nc.sync.dma_start(out=out_words[:, cols], in_=out_code[:, cols].bitcast(I32))

        for c in range(3):
            if c % 2 == 0:
                quantise("z1_%d" % c, z1_bf[c // 2][:], ((c, 0), (c + 1, 0)))
            z23 = extremes(c)
            quantise("z23_%d" % c, z23[:], ((c, 1), (c, 2)))
            product(c)
        hi = first_level(3, ALU.max, "hi")
        lo = first_level(3, ALU.min, "lo")
        z2 = sb("z2_last", [P, W], BF16)
        nc.vector.tensor_tensor(z2[:], hi[:, 0, :], hi[:, 1, :], ALU.max)
        z3 = sb("z3_last", [P, W], BF16)
        nc.vector.tensor_tensor(z3[:], lo[:, 0, :], lo[:, 1, :], ALU.min)
        quantise("z2_last", z2[:], ((3, 1),))
        quantise("z3_last", z3[:], ((3, 2),))
        planes(0)
        planes(1)
        weave(2, nc.vector.tensor_copy)
        planes(2)
        product(3)
        weave(3, nc.vector.tensor_copy)
        planes(3)
        for q in range(4):
            queue = nc.sync if q % 2 == 0 else nc.scalar
            queue.dma_start(out=out_2[0, 4 * q : 4 * q + 4, :].bitcast(I32), in_=out_scale[32 * q : 32 * q + 4, :].bitcast(I32))
